import numpy as np
import ml_dtypes


def mxq(x, axis, fmt="e4m3"):
    dtype, down = {"e4m3": (ml_dtypes.float8_e4m3fn, 7), "e5m2": (ml_dtypes.float8_e5m2, 14)}[fmt]
    v = np.moveaxis(np.asarray(x, np.float32).astype(ml_dtypes.bfloat16).astype(np.float64), axis, -1)
    blocks = v.reshape(v.shape[:-1] + (-1, 32))
    amax = np.abs(blocks).max(-1, keepdims=True)
    byte = np.maximum(np.where(amax > 0, np.frexp(amax)[1] - 1 + 127, 0) - down, 1)
    scale = np.exp2(byte - 127.0)
    codes = (blocks / scale).astype(np.float32).astype(dtype).astype(np.float64)
    return np.moveaxis((codes * scale).reshape(v.shape), -1, axis)


WIDE = False


def mx_kscale(k):
    if not WIDE:
        return np.ones(k)
    levels = np.array([10, -10, 5, -5, 0])
    if k % 512:
        return np.exp2(np.random.permutation(np.resize(levels, k // 32))).repeat(32)
    a = np.empty((k // 512, 16))
    for p in range(k // 512):
        a[p, :8] = np.random.permutation(np.resize(levels, 8))
        for g in range(8):
            far = levels[np.abs(levels - a[p, g]) >= 10]
            a[p, g + 8] = far[np.random.randint(len(far))]
    return np.exp2(a.ravel()).repeat(32)


def f64(x):
    return np.asarray(x).astype(np.float64)


def striped(idx):
    return np.tile(idx.reshape(-1, 16).T, (8, 1)).astype(np.uint16)


def unstriped(offs):
    return offs[:16].T.reshape(-1).astype(np.int64)


def pack_weight(w):
    k, n = w.shape
    w = f64(np.asarray(w, np.float32).astype(ml_dtypes.bfloat16)).reshape(k // 32, 32, n)
    amax = np.abs(w).max(1)
    byte = np.clip(np.where(amax > 0, np.frexp(amax)[1] - 1 + 127 - 7, 1), 1, 254)
    scaled = (w * np.exp2(127.0 - byte)[:, None, :]).reshape(k, n).astype(np.float32)
    words = np.ascontiguousarray(scaled.reshape(k // 512, 128, 4, n).transpose(0, 1, 3, 2)).astype(ml_dtypes.float8_e4m3fn).view(np.uint8)
    return words, np.ascontiguousarray(byte.astype(np.uint8).reshape(k // 512, 16, n))


def unpack_weight(words, scales):
    g, p, n, _ = words.shape
    vals = np.ascontiguousarray(words).view(ml_dtypes.float8_e4m3fn).astype(np.float64) * np.repeat(np.exp2(scales.astype(np.float64) - 127.0), 8, axis=1)[..., None]
    return vals.transpose(0, 1, 3, 2).reshape(g * 512, n)


def silu(v):
    return v / (1.0 + np.exp(-np.maximum(v, -700.0)))


K, T, N = 1536, 512, 256


def setup_inputs():
    n = np.random.standard_normal
    s = mx_kscale(K)[:, None]
    idx = np.random.permutation(K)
    x = n((T, K))
    x[:, idx] *= s[:, 0]
    words, scales = pack_weight(n((K, N)) / np.sqrt(K) / s)
    return {
        "x": x.astype(np.float32),
        "w_words": words,
        "w_scales": scales,
        "b": (0.3 * n((N, 1))).astype(np.float32),
        "offs": striped(idx),
    }


def reference(x, w_words, w_scales, b, offs):
    w = unpack_weight(w_words, w_scales)
    idx = unstriped(offs)
    xq = mxq(f64(x)[:, idx], 1, "e4m3").T
    return silu((w.T @ xq) + f64(b))

@@ -1,0 +1,138 @@
+from contextlib import ExitStack
+
+import concourse.mybir as mybir
+from concourse.masks import make_identity
+
+K, T, N = 1536, 512, 256
+FLOPS = 2 * K * T * N
+
+F32 = mybir.dt.float32
+BF16 = mybir.dt.bfloat16
+U32 = mybir.dt.uint32
+I32 = mybir.dt.int32
+U16 = mybir.dt.uint16
+U8 = mybir.dt.uint8
+FP8X4 = mybir.dt.float8_e4m3fn_x4
+COPY = mybir.ActivationFunctionType.Copy
+SILU = mybir.ActivationFunctionType.Silu
+MULT = mybir.AluOpType.mult
+ADD = mybir.AluOpType.add
+
+P = 128
+PASSES = K // 512
+HALVES = T // 256
+CH = 512
+
+
+def tile_picked_actorder_lin_silu_perm_l_kernel(tc, x, w_words, w_scales, b, offs, out):
+    nc = tc.nc
+    with ExitStack() as ctx:
+        keep = ctx.enter_context(tc.tile_pool(name="keep", bufs=1))
+        turn = ctx.enter_context(tc.psum_pool(name="turn", bufs=4))
+        accs = ctx.enter_context(tc.psum_pool(name="accs", bufs=1))
+
+        offsets = keep.tile([P, K // 16], U16, name="offsets")
+        ident = keep.tile([P, P], F32, name="ident")
+        w_codes = keep.tile([P, PASSES, N], U32, name="w_codes", align_bytes=64)
+        w_planes = keep.tile([P, PASSES, N], U8, name="w_planes", align_bytes=64)
+        bias = keep.tile([P, 2], F32, name="bias")
+        warm = keep.tile([P, 1], F32, name="warm")
+        warm2 = keep.tile([P, 1], F32, name="warm2")
+
+        raws = {}
+        pairs = []
+        for h in range(HALVES):
+            pairs.append(keep.tile([P, 2 * K], BF16, name=f"pairs{h}", align_bytes=64))
+            for c in range(K // CH):
+                raws[h, c] = keep.tile([P, 2, CH], F32, name=f"raw{h}_{c}")
+
+        def load_x(h, c):
+            nc.sync.dma_start(
+                raws[h, c][:],
+                x[256 * h : 256 * (h + 1), CH * c : CH * (c + 1)].rearrange("(e p) c -> p e c", e=2),
+            )
+
+        load_x(0, 0)
+        nc.sync.dma_start(offsets[:], offs)
+        load_x(0, 1)
+        load_x(0, 2)
+        load_x(1, 0)
+        load_x(1, 1)
+        load_x(1, 2)
+        nc.sync.dma_start(w_codes[:].bitcast(I32), w_words.rearrange("a p n r -> p a (n r)").bitcast(I32))
+        nc.vector.memset(w_planes[:].bitcast(U32), 0)
+        for q in range(4):
+            nc.sync.dma_start(
+                w_planes[32 * q : 32 * q + 4, :, :].bitcast(I32),
+                w_scales[:, 4 * q : 4 * q + 4, :].rearrange("a q n -> q a n").bitcast(I32),
+            )
+        nc.sync.dma_start(bias[:], b.rearrange("(m p) o -> p (m o)", p=P))
+
+        nc.vector.memset(warm[:], 0.0)
+        nc.scalar.activation(warm2[:], warm[:], SILU)
+        make_identity(nc, ident[:])
+
+        def cast(engine, h, c, lo, hi):
+            src = raws[h, c][:, :, lo:hi].rearrange("p e c -> p c e")
+            dst = pairs[h][:, 2 * (CH * c + lo) : 2 * (CH * c + hi)].rearrange("p (c e) -> p c e", e=2)
+            if engine == "v":
+                nc.vector.tensor_copy(dst, src)
+            elif engine == "s":
+                nc.scalar.copy(dst, src)
+            else:
+                nc.gpsimd.tensor_scalar(dst, src, 1.0, 0.0, MULT, ADD)
+
+        def acc_tile(h, m):
+            return accs.tile([P, 256], F32, name=f"acc{h}{m}")
+
+        acc = {(h, m): acc_tile(h, m) for h in range(HALVES) for m in range(2)}
+
+        def gather(h, g):
+            picked = keep.tile([P, 1024], BF16, name=f"picked{h}{g}", align_bytes=64)
+            nc.vector.tensor_copy(
+                picked[:].bitcast(U32).rearrange("p (t q) -> p q t", t=4),
+                pairs[h][:].bitcast(U32).indirect(offsets[:, 32 * g : 32 * (g + 1)]),
+            )
+            return picked
+
+        def rest(h, g, picked):
+            bank = turn.tile([P, 512], F32, name="bank")
+            words = picked[:].bitcast(F32)
+            for t in range(4):
+                nc.tensor.transpose(bank[:, P * t : P * (t + 1)], words[:, P * t : P * (t + 1)], ident[:])
+            grouped = keep.tile([P, 1024], BF16, name=f"grouped{h}{g}", align_bytes=64)
+            src = bank[:].bitcast(BF16).rearrange("p (t q e) -> p e q t", t=4, e=2)
+            dst = grouped[:].rearrange("p (e q t) -> p e q t", e=2, t=4)
+            nc.scalar.copy(dst, src)
+            codes = keep.tile([P, 256], U32, name=f"codes{h}{g}", align_bytes=64)
+            planes = keep.tile([P, 256], U8, name=f"planes{h}{g}", align_bytes=64)
+            nc.vector.quantize_mx(out=codes[:].bitcast(FP8X4), scales=planes[:], in_=grouped[:])
+            for m in range(2):
+                cols = slice(P * m, P * (m + 1))
+                nc.tensor.matmul_mx(
+                    out=acc[h, m][:],
+                    lhsT=w_codes[:, g, cols].bitcast(FP8X4),
+                    lhsT_scale=w_planes[:, g, cols],
+                    rhs=codes[:].bitcast(FP8X4),
+                    rhs_scale=planes[:],
+                    start=(g == 0),
+                    stop=(g == PASSES - 1),
+                )
+
+        cast("v", 0, 0, 0, CH)
+        cast("v", 0, 1, 0, CH)
+        cast("v", 0, 2, 0, 320)
+        cast("s", 0, 2, 320, CH)
+        cast("s", 1, 0, 0, CH)
+        cast("g", 1, 1, 0, CH)
+        cast("s", 1, 2, 0, 256)
+        cast("g", 1, 2, 256, CH)
+
+        for h in range(HALVES):
+            for g in range(PASSES):
+                picked = gather(h, g)
+                rest(h, g, picked)
+            for m in range(2):
+                y = keep.tile([P, 256], F32, name=f"y{h}{m}")
+                nc.scalar.activation(y[:], acc[h, m][:], SILU, bias=bias[:, m : m + 1])
+                nc.sync.dma_start(out[P * m : P * (m + 1), 256 * h : 256 * (h + 1)], y[:])

@@ -21,7 +21,7 @@ ADD = mybir.AluOpType.add
 P = 128
 PASSES = K // 512
 HALVES = T // 256
-CH = 512
+CUTS = [[0, 576, 1152, 1536], [0, 512, 1024, 1536]]
 
 
 def tile_picked_actorder_lin_silu_perm_l_kernel(tc, x, w_words, w_scales, b, offs, out):
@@ -43,13 +43,13 @@ def tile_picked_actorder_lin_silu_perm_l_kernel(tc, x, w_words, w_scales, b, off
         pairs = []
         for h in range(HALVES):
             pairs.append(keep.tile([P, 2 * K], BF16, name=f"pairs{h}", align_bytes=64))
-            for c in range(K // CH):
-                raws[h, c] = keep.tile([P, 2, CH], F32, name=f"raw{h}_{c}")
+            for c in range(3):
+                raws[h, c] = keep.tile([P, 2, CUTS[h][c + 1] - CUTS[h][c]], F32, name=f"raw{h}_{c}")
 
         def load_x(h, c):
             nc.sync.dma_start(
                 raws[h, c][:],
-                x[256 * h : 256 * (h + 1), CH * c : CH * (c + 1)].rearrange("(e p) c -> p e c", e=2),
+                x[256 * h : 256 * (h + 1), CUTS[h][c] : CUTS[h][c + 1]].rearrange("(e p) c -> p e c", e=2),
             )
 
         load_x(0, 0)
@@ -74,7 +74,7 @@ def tile_picked_actorder_lin_silu_perm_l_kernel(tc, x, w_words, w_scales, b, off
 
         def cast(engine, h, c, lo, hi):
             src = raws[h, c][:, :, lo:hi].rearrange("p e c -> p c e")
-            dst = pairs[h][:, 2 * (CH * c + lo) : 2 * (CH * c + hi)].rearrange("p (c e) -> p c e", e=2)
+            dst = pairs[h][:, 2 * (CUTS[h][c] + lo) : 2 * (CUTS[h][c] + hi)].rearrange("p (c e) -> p c e", e=2)
             if engine == "v":
                 nc.vector.tensor_copy(dst, src)
             elif engine == "s":
@@ -95,18 +95,29 @@ def tile_picked_actorder_lin_silu_perm_l_kernel(tc, x, w_words, w_scales, b, off
             )
             return picked
 
-        def rest(h, g, picked):
+        grouped = {}
+
+        def turn_over(h, g):
             bank = turn.tile([P, 512], F32, name="bank")
-            words = picked[:].bitcast(F32)
+            words = picks[h, g][:].bitcast(F32)
             for t in range(4):
                 nc.tensor.transpose(bank[:, P * t : P * (t + 1)], words[:, P * t : P * (t + 1)], ident[:])
-            grouped = keep.tile([P, 1024], BF16, name=f"grouped{h}{g}", align_bytes=64)
             src = bank[:].bitcast(BF16).rearrange("p (t q e) -> p e q t", t=4, e=2)
-            dst = grouped[:].rearrange("p (e q t) -> p e q t", e=2, t=4)
-            nc.scalar.copy(dst, src)
+            grouped[h, g] = keep.tile([P, 1024], BF16, name=f"grouped{h}{g}", align_bytes=64)
+            dst = grouped[h, g][:].rearrange("p (e q t) -> p e q t", e=2, t=4)
+            if (h, g) in [(1, 2)]:
+                for e in range(2):
+                    nc.scalar.copy(dst[:, e], src[:, e])
+            else:
+                nc.scalar.copy(dst, src)
+
+        def multiply(h, g):
             codes = keep.tile([P, 256], U32, name=f"codes{h}{g}", align_bytes=64)
             planes = keep.tile([P, 256], U8, name=f"planes{h}{g}", align_bytes=64)
-            nc.vector.quantize_mx(out=codes[:].bitcast(FP8X4), scales=planes[:], in_=grouped[:])
+            for e in range(2) if (h, g) in [(1, 2)] else [slice(0, 2)]:
+                lo, hi = (e.start, e.stop) if (h, g) not in [(1, 2)] else (e, e + 1)
+                half = slice(P * lo, P * hi)
+                nc.vector.quantize_mx(out=codes[:, half].bitcast(FP8X4), scales=planes[:, half], in_=grouped[h, g][:, 512 * lo : 512 * hi])
             for m in range(2):
                 cols = slice(P * m, P * (m + 1))
                 nc.tensor.matmul_mx(
@@ -119,19 +130,25 @@ def tile_picked_actorder_lin_silu_perm_l_kernel(tc, x, w_words, w_scales, b, off
                     stop=(g == PASSES - 1),
                 )
 
-        cast("v", 0, 0, 0, CH)
-        cast("v", 0, 1, 0, CH)
-        cast("v", 0, 2, 0, 320)
-        cast("s", 0, 2, 320, CH)
-        cast("s", 1, 0, 0, CH)
-        cast("g", 1, 1, 0, CH)
-        cast("s", 1, 2, 0, 256)
-        cast("g", 1, 2, 256, CH)
+        cast("v", 0, 0, 0, 576)
+        cast("v", 0, 1, 0, 576)
+        cast("v", 0, 2, 0, 256)
+        cast("s", 0, 2, 256, 384)
+        cast("s", 1, 0, 0, 256)
+        cast("g", 1, 0, 256, 512)
+        cast("g", 1, 1, 0, 512)
+        cast("g", 1, 2, 128, 512)
 
+        picks = {(0, g): gather(0, g) for g in range(PASSES)}
+        cast("v", 1, 2, 0, 128)
+        for g in range(PASSES):
+            picks[1, g] = gather(1, g)
         for h in range(HALVES):
             for g in range(PASSES):
-                picked = gather(h, g)
-                rest(h, g, picked)
+                turn_over(h, g)
+        for h in range(HALVES):
+            for g in range(PASSES):
+                multiply(h, g)
             for m in range(2):
                 y = keep.tile([P, 256], F32, name=f"y{h}{m}")
                 nc.scalar.activation(y[:], acc[h, m][:], SILU, bias=bias[:, m : m + 1])

@@ -21,7 +21,7 @@ ADD = mybir.AluOpType.add
 P = 128
 PASSES = K // 512
 HALVES = T // 256
-CUTS = [[0, 576, 1152, 1536], [0, 512, 1024, 1536]]
+CUTS = [[0, 576, 1152, 1536], [0, 576, 1152, 1536]]
 
 
 def tile_picked_actorder_lin_silu_perm_l_kernel(tc, x, w_words, w_scales, b, offs, out):
@@ -89,8 +89,9 @@ def tile_picked_actorder_lin_silu_perm_l_kernel(tc, x, w_words, w_scales, b, off
 
         def gather(h, g):
             picked = keep.tile([P, 1024], BF16, name=f"picked{h}{g}", align_bytes=64)
+            words = picked[:].bitcast(U32)
             nc.vector.tensor_copy(
-                picked[:].bitcast(U32).rearrange("p (t q) -> p q t", t=4),
+                words.rearrange("p (t q) -> p q t", t=4) if (h, g) == (1, 2) else words,
                 pairs[h][:].bitcast(U32).indirect(offsets[:, 32 * g : 32 * (g + 1)]),
             )
             return picked
@@ -101,7 +102,7 @@ def tile_picked_actorder_lin_silu_perm_l_kernel(tc, x, w_words, w_scales, b, off
             bank = turn.tile([P, 512], F32, name="bank")
             words = picks[h, g][:].bitcast(F32)
             for t in range(4):
-                nc.tensor.transpose(bank[:, P * t : P * (t + 1)], words[:, P * t : P * (t + 1)], ident[:])
+                nc.tensor.transpose(bank[:, P * t : P * (t + 1)], words[:, P * t : P * (t + 1)] if (h, g) == (1, 2) else words[:, t : 512 : 4], ident[:])
             src = bank[:].bitcast(BF16).rearrange("p (t q e) -> p e q t", t=4, e=2)
             grouped[h, g] = keep.tile([P, 1024], BF16, name=f"grouped{h}{g}", align_bytes=64)
             dst = grouped[h, g][:].rearrange("p (e q t) -> p e q t", e=2, t=4)
@@ -134,13 +135,13 @@ def tile_picked_actorder_lin_silu_perm_l_kernel(tc, x, w_words, w_scales, b, off
         cast("v", 0, 1, 0, 576)
         cast("v", 0, 2, 0, 256)
         cast("s", 0, 2, 256, 384)
-        cast("s", 1, 0, 0, 256)
-        cast("g", 1, 0, 256, 512)
-        cast("g", 1, 1, 0, 512)
-        cast("g", 1, 2, 128, 512)
+        cast("s", 1, 0, 0, 576)
+        cast("s", 1, 1, 0, 192)
+        cast("s", 1, 2, 0, 256)
 
         picks = {(0, g): gather(0, g) for g in range(PASSES)}
-        cast("v", 1, 2, 0, 128)
+        cast("v", 1, 1, 192, 576)
+        cast("v", 1, 2, 256, 384)
         for g in range(PASSES):
             picks[1, g] = gather(1, g)
         for h in range(HALVES):

from contextlib import ExitStack

import concourse.mybir as mybir
from concourse.masks import make_identity

K, T, N = 1536, 512, 256
FLOPS = 2 * K * T * N

F32 = mybir.dt.float32
BF16 = mybir.dt.bfloat16
U32 = mybir.dt.uint32
I32 = mybir.dt.int32
U16 = mybir.dt.uint16
U8 = mybir.dt.uint8
FP8X4 = mybir.dt.float8_e4m3fn_x4
COPY = mybir.ActivationFunctionType.Copy
SILU = mybir.ActivationFunctionType.Silu
MULT = mybir.AluOpType.mult
ADD = mybir.AluOpType.add

P = 128
PASSES = K // 512
HALVES = T // 256
CUTS = [[0, 576, 1152, 1536], [0, 576, 1152, 1536]]


def tile_picked_actorder_lin_silu_perm_l_kernel(tc, x, w_words, w_scales, b, offs, out):
    nc = tc.nc
    with ExitStack() as ctx:
        keep = ctx.enter_context(tc.tile_pool(name="keep", bufs=1))
        turn = ctx.enter_context(tc.psum_pool(name="turn", bufs=4))
        accs = ctx.enter_context(tc.psum_pool(name="accs", bufs=1))

        offsets = keep.tile([P, K // 16], U16, name="offsets")
        ident = keep.tile([P, P], F32, name="ident")
        w_codes = keep.tile([P, PASSES, N], U32, name="w_codes", align_bytes=64)
        w_planes = keep.tile([P, PASSES, N], U8, name="w_planes", align_bytes=64)
        bias = keep.tile([P, 2], F32, name="bias")
        warm = keep.tile([P, 1], F32, name="warm")
        warm2 = keep.tile([P, 1], F32, name="warm2")

        raws = {}
        pairs = []
        for h in range(HALVES):
            pairs.append(keep.tile([P, 2 * K], BF16, name=f"pairs{h}", align_bytes=64))
            for c in range(3):
                raws[h, c] = keep.tile([P, 2, CUTS[h][c + 1] - CUTS[h][c]], F32, name=f"raw{h}_{c}")

        def load_x(h, c):
            nc.sync.dma_start(
                raws[h, c][:],
                x[256 * h : 256 * (h + 1), CUTS[h][c] : CUTS[h][c + 1]].rearrange("(e p) c -> p e c", e=2),
            )

        load_x(0, 0)
        nc.sync.dma_start(offsets[:], offs)
        load_x(0, 1)
        load_x(0, 2)
        load_x(1, 0)
        load_x(1, 1)
        load_x(1, 2)
        nc.sync.dma_start(w_codes[:].bitcast(I32), w_words.rearrange("a p n r -> p a (n r)").bitcast(I32))
        nc.vector.memset(w_planes[:].bitcast(U32), 0)
        for q in range(4):
            nc.sync.dma_start(
                w_planes[32 * q : 32 * q + 4, :, :].bitcast(I32),
                w_scales[:, 4 * q : 4 * q + 4, :].rearrange("a q n -> q a n").bitcast(I32),
            )
        nc.sync.dma_start(bias[:], b.rearrange("(m p) o -> p (m o)", p=P))

        nc.vector.memset(warm[:], 0.0)
        nc.scalar.activation(warm2[:], warm[:], SILU)
        make_identity(nc, ident[:])

        def cast(engine, h, c, lo, hi):
            src = raws[h, c][:, :, lo:hi].rearrange("p e c -> p c e")
            dst = pairs[h][:, 2 * (CUTS[h][c] + lo) : 2 * (CUTS[h][c] + hi)].rearrange("p (c e) -> p c e", e=2)
            if engine == "v":
                nc.vector.tensor_copy(dst, src)
            elif engine == "s":
                nc.scalar.copy(dst, src)
            else:
                nc.gpsimd.tensor_scalar(dst, src, 1.0, 0.0, MULT, ADD)

        def acc_tile(h, m):
            return accs.tile([P, 256], F32, name=f"acc{h}{m}")

        acc = {(h, m): acc_tile(h, m) for h in range(HALVES) for m in range(2)}

        def gather(h, g):
            picked = keep.tile([P, 1024], BF16, name=f"picked{h}{g}", align_bytes=64)
            words = picked[:].bitcast(U32)
            nc.vector.tensor_copy(
                words.rearrange("p (t q) -> p q t", t=4) if (h, g) == (1, 2) else words,
                pairs[h][:].bitcast(U32).indirect(offsets[:, 32 * g : 32 * (g + 1)]),
            )
            return picked

        grouped = {}

        def turn_over(h, g):
            bank = turn.tile([P, 512], F32, name="bank")
            words = picks[h, g][:].bitcast(F32)
            for t in range(4):
                nc.tensor.transpose(bank[:, P * t : P * (t + 1)], words[:, P * t : P * (t + 1)] if (h, g) == (1, 2) else words[:, t : 512 : 4], ident[:])
            src = bank[:].bitcast(BF16).rearrange("p (t q e) -> p e q t", t=4, e=2)
            grouped[h, g] = keep.tile([P, 1024], BF16, name=f"grouped{h}{g}", align_bytes=64)
            dst = grouped[h, g][:].rearrange("p (e q t) -> p e q t", e=2, t=4)
            if (h, g) in [(1, 2)]:
                for e in range(2):
                    nc.scalar.copy(dst[:, e], src[:, e])
            else:
                nc.scalar.copy(dst, src)

        def multiply(h, g):
            codes = keep.tile([P, 256], U32, name=f"codes{h}{g}", align_bytes=64)
            planes = keep.tile([P, 256], U8, name=f"planes{h}{g}", align_bytes=64)
            for e in range(2) if (h, g) in [(1, 2)] else [slice(0, 2)]:
                lo, hi = (e.start, e.stop) if (h, g) not in [(1, 2)] else (e, e + 1)
                half = slice(P * lo, P * hi)
                nc.vector.quantize_mx(out=codes[:, half].bitcast(FP8X4), scales=planes[:, half], in_=grouped[h, g][:, 512 * lo : 512 * hi])
            for m in range(2):
                cols = slice(P * m, P * (m + 1))
                nc.tensor.matmul_mx(
                    out=acc[h, m][:],
                    lhsT=w_codes[:, g, cols].bitcast(FP8X4),
                    lhsT_scale=w_planes[:, g, cols],
                    rhs=codes[:].bitcast(FP8X4),
                    rhs_scale=planes[:],
                    start=(g == 0),
                    stop=(g == PASSES - 1),
                )

        cast("v", 0, 0, 0, 576)
        cast("v", 0, 1, 0, 576)
        cast("v", 0, 2, 0, 256)
        cast("s", 0, 2, 256, 384)
        cast("s", 1, 0, 0, 576)
        cast("s", 1, 1, 0, 192)
        cast("s", 1, 2, 0, 256)

        picks = {(0, g): gather(0, g) for g in range(PASSES)}
        cast("v", 1, 1, 192, 576)
        cast("v", 1, 2, 256, 384)
        for g in range(PASSES):
            picks[1, g] = gather(1, g)
        for h in range(HALVES):
            for g in range(PASSES):
                turn_over(h, g)
        for h in range(HALVES):
            for g in range(PASSES):
                multiply(h, g)
            for m in range(2):
                y = keep.tile([P, 256], F32, name=f"y{h}{m}")
                nc.scalar.activation(y[:], acc[h, m][:], SILU, bias=bias[:, m : m + 1])
                nc.sync.dma_start(out[P * m : P * (m + 1), 256 * h : 256 * (h + 1)], y[:])
